import numpy as np
import ml_dtypes


def mxq(x, axis, fmt="e4m3"):
    dtype, down = {"e4m3": (ml_dtypes.float8_e4m3fn, 7), "e5m2": (ml_dtypes.float8_e5m2, 14)}[fmt]
    v = np.moveaxis(np.asarray(x, np.float32).astype(ml_dtypes.bfloat16).astype(np.float64), axis, -1)
    blocks = v.reshape(v.shape[:-1] + (-1, 32))
    amax = np.abs(blocks).max(-1, keepdims=True)
    byte = np.maximum(np.where(amax > 0, np.frexp(amax)[1] - 1 + 127, 0) - down, 1)
    scale = np.exp2(byte - 127.0)
    codes = (blocks / scale).astype(np.float32).astype(dtype).astype(np.float64)
    return np.moveaxis((codes * scale).reshape(v.shape), -1, axis)


WIDE = False


def mx_kscale(k):
    if not WIDE:
        return np.ones(k)
    levels = np.array([10, -10, 5, -5, 0])
    if k % 512:
        return np.exp2(np.random.permutation(np.resize(levels, k // 32))).repeat(32)
    a = np.empty((k // 512, 16))
    for p in range(k // 512):
        a[p, :8] = np.random.permutation(np.resize(levels, 8))
        for g in range(8):
            far = levels[np.abs(levels - a[p, g]) >= 10]
            a[p, g + 8] = far[np.random.randint(len(far))]
    return np.exp2(a.ravel()).repeat(32)


def f64(x):
    return np.asarray(x).astype(np.float64)


def planes(y):
    n, m = y.shape
    v = y.astype(np.float32).astype(ml_dtypes.bfloat16).astype(np.float64).reshape(n // 32, 32, m)
    top = np.abs(v).max(1)
    byte = np.clip(np.where(top > 0, np.frexp(top)[1] - 1 + 127 - 7, 1), 1, 254)
    codes = (v * np.exp2(127.0 - byte)[:, None, :]).reshape(n, m).astype(np.float32).astype(ml_dtypes.float8_e4m3fn).view(np.uint8)
    words = codes.reshape(n // 512, 128, 4, m).transpose(0, 1, 3, 2)
    return np.ascontiguousarray(words), np.ascontiguousarray(byte.astype(np.uint8).reshape(n // 512, 16, m))


def split(x):
    m, e = np.frexp(f64(x))
    hi = np.ldexp(np.trunc(16.0 * m) / 16.0, e)
    return hi, f64(x) - hi


def silu(v):
    return v / (1.0 + np.exp(-np.maximum(v, -700.0)))


K, M, T = 1024, 512, 1536


def setup_inputs():
    n = np.random.standard_normal
    s = mx_kscale(K)[:, None]
    return {
        "w": (n((K, M)) / np.sqrt(K) / s).astype(np.float32),
        "x": (n((K, T)) * s).astype(np.float32),
        "b": (0.3 * n(512)).astype(np.float32),
    }


def reference(w, x, b):
    w_hi, w_lo = split(w)
    w_hi_, w_lo_ = mxq(w_hi, 0, "e4m3"), mxq(w_lo, 0, "e4m3")
    x_hi, x_lo = split(x)
    x_hi_, x_lo_ = mxq(x_hi, 0, "e4m3"), mxq(x_lo, 0, "e4m3")
    y = w_hi_.T @ x_hi_ + w_hi_.T @ x_lo_ + w_lo_.T @ x_hi_
    out_0 = silu(y + f64(b)[:, None])
    return (out_0,) + planes(out_0)

@@ -1,0 +1,207 @@
+from contextlib import ExitStack
+
+import concourse.mybir as mybir
+
+K, M, T = 1024, 512, 1536
+FLOPS = 3 * 2 * K * M * T
+
+F32 = mybir.dt.float32
+BF16 = mybir.dt.bfloat16
+I32 = mybir.dt.int32
+U32 = mybir.dt.uint32
+U8 = mybir.dt.uint8
+FP8X4 = mybir.dt.float8_e4m3fn_x4
+ALU = mybir.AluOpType
+SILU = mybir.ActivationFunctionType.Silu
+
+P = 128
+PACK = 4
+K_PASS = P * PACK
+PASSES = K // K_PASS
+RUN = 4
+HI_MASK = 0xFFF0FFF0 - (1 << 32)
+W_PARTS = [[128, 128, 256], [256, 256]]
+CHUNKS = [512, 512, 256, 128, 128]
+SLAB_COLS = 512
+
+
+def tile_mix_split3_fm_pl_silu_kernel(tc, w, x, b, out_0, out_1, out_2):
+    nc = tc.nc
+    y_rows = out_0.rearrange("(p t) c -> p t c", t=PACK)
+    words_out = out_1[0].rearrange("p c i -> p (c i)").bitcast(I32)
+    scales_out = out_2[0].bitcast(I32)
+
+    with ExitStack() as ctx:
+        keep = ctx.enter_context(tc.tile_pool(name="keep", bufs=1))
+        psum = ctx.enter_context(tc.psum_pool(name="psum", bufs=2))
+        ctx.enter_context(tc.manual_schedule())
+
+        def new_slab(name, cols):
+            slab = {"cols": cols, "parts": []}
+            for half in ("hi", "lo"):
+                slab[half] = keep.tile([P, cols * PACK], BF16, name=name + half, align_bytes=256)
+                slab[half + "_codes"] = keep.tile([P, cols], U32, name=name + half + "c", align_bytes=256)
+                slab[half + "_scales"] = keep.tile([P, cols], U8, name=name + half + "s", align_bytes=256)
+            return slab
+
+        def rows(src, g, c0, width):
+            return src[g * K_PASS : (g + 1) * K_PASS, c0 : c0 + width].rearrange("(p j) c -> p j c", j=PACK)
+
+        slabs = []
+        w_slabs = []
+        for g in range(PASSES):
+            slab = new_slab("w%d" % g, M)
+            c0 = 0
+            for width in W_PARTS[g]:
+                raw = keep.tile([P, PACK, width], F32, name="w%d_%d" % (g, c0), align_bytes=256)
+                nc.sync.dma_start(out=raw[:], in_=rows(w, g, c0, width))
+                m = slice(c0 // PACK, (c0 + width) // PACK)
+                upper = raw[:].bitcast(BF16).rearrange("p j (m t two) -> p m j t two", t=PACK, two=2)[:, :, :, :, 1]
+                hi = slab["hi"][:].rearrange("p (t m j) -> p m j t", t=PACK, j=PACK)[:, m]
+                lo = slab["lo"][:].rearrange("p (t m j) -> p m j t", t=PACK, j=PACK)[:, m]
+                full = raw[:].rearrange("p j (m t) -> p m j t", t=PACK)
+                pairs = slab["hi"][:].bitcast(I32).rearrange("p (t m h) -> p t m h", t=PACK, h=2)[:, :, m, :]
+                subs = [(lo[:, :, :, t : t + 2], full[:, :, :, t : t + 2], hi[:, :, :, t : t + 2]) for t in (0, 2)]
+                slab["parts"].append({"upper": upper, "hi": hi, "pairs": pairs, "subs": subs})
+                c0 += width
+            slabs.append(slab)
+            w_slabs.append(slab)
+
+        bias = keep.tile([P, PACK], F32)
+        nc.sync.dma_start(out=bias[:], in_=b.rearrange("(p t) -> p t", t=PACK))
+
+        chunks = []
+        c0 = 0
+        for c, width in enumerate(CHUNKS):
+            groups = [[g] for g in range(PASSES)] if width == SLAB_COLS else [list(range(PASSES))]
+            chunk = {"c0": c0, "width": width, "slabs": []}
+            for gs in groups:
+                name = "x%d_%d" % (c, gs[0])
+                slab = new_slab(name, width * len(gs))
+                raw = keep.tile([P, PACK, len(gs), width], F32, name=name + "raw", align_bytes=256)
+                for n, g in enumerate(gs):
+                    nc.sync.dma_start(out=raw[:, :, n, :], in_=rows(x, g, c0, width))
+                flat = raw[:].rearrange("p j g c -> p j (g c)")
+                upper = flat.bitcast(BF16).rearrange("p j (c i two) -> p c j i two", i=RUN, two=2)[:, :, :, :, 1]
+                hi = slab["hi"][:].rearrange("p (c i j) -> p c j i", i=RUN, j=PACK)
+                lo = slab["lo"][:].rearrange("p (c i j) -> p c j i", i=RUN, j=PACK)
+                full = flat.rearrange("p j (c i) -> p c j i", i=RUN)
+                slab["parts"].append({"upper": upper, "hi": hi, "pairs": slab["hi"][:].bitcast(I32), "subs": [(lo, full, hi)]})
+                slab["passes"] = gs
+                slab["chunk"] = c
+                slabs.append(slab)
+                chunk["slabs"].append(slab)
+            chunk["y"] = keep.tile([P, PACK, width], F32, name="y%d" % c, align_bytes=256)
+            chunk["y16"] = keep.tile([P, width * PACK], BF16, name="y16_%d" % c, align_bytes=256)
+            chunk["codes"] = keep.tile([P, width], U32, name="yc%d" % c, align_bytes=256)
+            chunks.append(chunk)
+            c0 += width
+        y_scales = keep.tile([P, T], U8, align_bytes=256)
+
+        warm_in = keep.tile([P, 1], F32)
+        warm_out = keep.tile([P, 1], F32)
+        nc.gpsimd.memset(warm_in[:], 0.0)
+        nc.scalar.activation(out=warm_out[:], in_=warm_in[:], func=SILU)
+
+        def take_upper(slab):
+            for part in slab["parts"]:
+                nc.scalar.copy(out=part["hi"], in_=part["upper"])
+
+        def mask(part):
+            nc.vector.tensor_scalar(out=part["pairs"], in0=part["pairs"], scalar1=HI_MASK, scalar2=None, op0=ALU.bitwise_and)
+
+        def subtract(sub):
+            nc.vector.tensor_tensor(out=sub[0], in0=sub[1], in1=sub[2], op=ALU.subtract)
+
+        def multiply(slab, half):
+            chunk = chunks[slab["chunk"]]
+            width = chunk["width"]
+            if half == "hi" and slab["passes"][0] == 0:
+                chunk["acc"] = []
+                for t in range(PACK):
+                    acc = psum.tile([P, SLAB_COLS], F32, name="acc%d" % t)
+                    chunk["acc"].append(acc)
+            w_halves = ("hi", "lo") if half == "hi" else ("hi",)
+            for t in range(PACK):
+                n_cols = slice(t * P, (t + 1) * P)
+                for n, g in enumerate(slab["passes"]):
+                    t_cols = slice(n * width, (n + 1) * width)
+                    for w_half in w_halves:
+                        nc.tensor.matmul_mx(
+                            out=chunk["acc"][t][:, :width],
+                            lhsT=w_slabs[g][w_half + "_codes"][:, n_cols].bitcast(FP8X4),
+                            lhsT_scale=w_slabs[g][w_half + "_scales"][:, n_cols],
+                            rhs=slab[half + "_codes"][:, t_cols].bitcast(FP8X4),
+                            rhs_scale=slab[half + "_scales"][:, t_cols],
+                            start=(g == 0 and half == "hi" and w_half == "hi"),
+                            stop=(g == PASSES - 1 and half == "lo"),
+                        )
+
+        def quantize(slab, half):
+            nc.vector.quantize_mx(out=slab[half + "_codes"][:].bitcast(FP8X4), scales=slab[half + "_scales"][:], in_=slab[half][:])
+            if "chunk" in slab:
+                multiply(slab, half)
+
+        def activate(c):
+            chunk = chunks[c]
+            for t in range(PACK):
+                nc.scalar.activation(out=chunk["y"][:, t, :], in_=chunk["acc"][t][:, : chunk["width"]], func=SILU, bias=bias[:, t : t + 1])
+            nc.sync.dma_start(out=y_rows[:, :, chunk["c0"] : chunk["c0"] + chunk["width"]], in_=chunk["y"][:])
+
+        def round_y(c, copy):
+            chunk = chunks[c]
+            copy(
+                out=chunk["y16"][:].rearrange("p (c i t) -> p c t i", i=RUN, t=PACK),
+                in_=chunk["y"][:].rearrange("p t (c i) -> p c t i", i=RUN),
+            )
+
+        def quantize_y(c):
+            chunk = chunks[c]
+            cols = slice(chunk["c0"], chunk["c0"] + chunk["width"])
+            nc.vector.quantize_mx(out=chunk["codes"][:].bitcast(FP8X4), scales=y_scales[:, cols], in_=chunk["y16"][:])
+            nc.sync.dma_start(out=words_out[:, cols], in_=chunk["codes"][:].bitcast(I32))
+
+        late = chunks[3]["slabs"] + chunks[4]["slabs"]
+        for slab in slabs[: len(slabs) - len(late)]:
+            take_upper(slab)
+
+        mask(slabs[0]["parts"][0])
+        for s, slab in enumerate(slabs):
+            parts = slab["parts"]
+            for n, part in enumerate(parts):
+                last = n == len(parts) - 1
+                for sub in part["subs"][:-1]:
+                    subtract(sub)
+                if not last:
+                    mask(parts[n + 1])
+                subtract(part["subs"][-1])
+                if n == len(parts) - 2:
+                    quantize(slab, "hi")
+            following = slabs[s + 1] if s + 1 < len(slabs) else None
+            if following is not None:
+                mask(following["parts"][0])
+            quantize(slab, "lo")
+            closed = slab["chunk"] if "chunk" in slab and slab["passes"][-1] == PASSES - 1 else None
+            if closed is not None:
+                activate(closed)
+            if closed == 0:
+                for late_slab in late:
+                    take_upper(late_slab)
+                round_y(0, nc.scalar.copy)
+            if closed == 1:
+                quantize_y(0)
+                round_y(1, nc.scalar.copy)
+            if closed == 3:
+                round_y(2, nc.scalar.copy)
+            if following is not None and len(following["parts"]) == 1:
+                quantize(following, "hi")
+
+        quantize_y(1)
+        round_y(3, nc.vector.tensor_copy)
+        quantize_y(2)
+        quantize_y(3)
+        round_y(4, nc.vector.tensor_copy)
+        quantize_y(4)
+        for q in range(4):
+            queue = nc.sync if q % 2 == 0 else nc.scalar
+            queue.dma_start(out=scales_out[4 * q : 4 * q + 4, :], in_=y_scales[32 * q : 32 * q + 4, :].bitcast(I32))

@@ -20,7 +20,7 @@ K_PASS = P * PACK
 PASSES = K // K_PASS
 RUN = 4
 HI_MASK = 0xFFF0FFF0 - (1 << 32)
-W_PARTS = [[128, 128, 256], [256, 256]]
+W_UNIT = [128, 256]
 CHUNKS = [512, 512, 256, 128, 128]
 SLAB_COLS = 512
 
@@ -37,7 +37,7 @@ def tile_mix_split3_fm_pl_silu_kernel(tc, w, x, b, out_0, out_1, out_2):
         ctx.enter_context(tc.manual_schedule())
 
         def new_slab(name, cols):
-            slab = {"cols": cols, "parts": []}
+            slab = {"cols": cols}
             for half in ("hi", "lo"):
                 slab[half] = keep.tile([P, cols * PACK], BF16, name=name + half, align_bytes=256)
                 slab[half + "_codes"] = keep.tile([P, cols], U32, name=name + half + "c", align_bytes=256)
@@ -47,55 +47,70 @@ def tile_mix_split3_fm_pl_silu_kernel(tc, w, x, b, out_0, out_1, out_2):
         def rows(src, g, c0, width):
             return src[g * K_PASS : (g + 1) * K_PASS, c0 : c0 + width].rearrange("(p j) c -> p j c", j=PACK)
 
-        slabs = []
-        w_slabs = []
-        for g in range(PASSES):
-            slab = new_slab("w%d" % g, M)
-            c0 = 0
-            for width in W_PARTS[g]:
-                raw = keep.tile([P, PACK, width], F32, name="w%d_%d" % (g, c0), align_bytes=256)
-                nc.sync.dma_start(out=raw[:], in_=rows(w, g, c0, width))
-                m = slice(c0 // PACK, (c0 + width) // PACK)
-                upper = raw[:].bitcast(BF16).rearrange("p j (m t two) -> p m j t two", t=PACK, two=2)[:, :, :, :, 1]
+        def w_load(g, c0, width):
+            raw = keep.tile([P, PACK, width], F32, name="w%d_%d" % (g, c0), align_bytes=256)
+            nc.sync.dma_start(out=raw[:], in_=rows(w, g, c0, width))
+            slab = w_slabs[g]
+            step = W_UNIT[g]
+            for u0 in range(0, width, step):
+                m = slice((c0 + u0) // PACK, (c0 + u0 + step) // PACK)
+                src = raw[:, :, u0 : u0 + step]
+                upper = src.bitcast(BF16).rearrange("p j (m t two) -> p m j t two", t=PACK, two=2)[:, :, :, :, 1]
+                full = src.rearrange("p j (m t) -> p m j t", t=PACK)
                 hi = slab["hi"][:].rearrange("p (t m j) -> p m j t", t=PACK, j=PACK)[:, m]
                 lo = slab["lo"][:].rearrange("p (t m j) -> p m j t", t=PACK, j=PACK)[:, m]
-                full = raw[:].rearrange("p j (m t) -> p m j t", t=PACK)
                 pairs = slab["hi"][:].bitcast(I32).rearrange("p (t m h) -> p t m h", t=PACK, h=2)[:, :, m, :]
                 subs = [(lo[:, :, :, t : t + 2], full[:, :, :, t : t + 2], hi[:, :, :, t : t + 2]) for t in (0, 2)]
-                slab["parts"].append({"upper": upper, "hi": hi, "pairs": pairs, "subs": subs})
-                c0 += width
-            slabs.append(slab)
-            w_slabs.append(slab)
+                done = c0 + u0 + step == M
+                units.append({"upper": upper, "hi": hi, "pairs": pairs, "subs": subs, "slab": slab, "cols": slice(0, M) if done else None, "done": done})
 
-        bias = keep.tile([P, PACK], F32)
-        nc.sync.dma_start(out=bias[:], in_=b.rearrange("(p t) -> p t", t=PACK))
+        def x_load(slab, c0, width):
+            chunk = chunks[slab["chunk"]]
+            gs = slab["passes"]
+            raw = keep.tile([P, PACK, len(gs), width], F32, name="x%d_%d" % (gs[0], chunk["c0"] + c0), align_bytes=256)
+            for n, g in enumerate(gs):
+                nc.sync.dma_start(out=raw[:, :, n, :], in_=rows(x, g, chunk["c0"] + c0, width))
+            cols = slice(c0, c0 + width * len(gs))
+            elems = slice(cols.start * PACK, cols.stop * PACK)
+            flat = raw[:].rearrange("p j g c -> p j (g c)")
+            upper = flat.bitcast(BF16).rearrange("p j (c i two) -> p c j i two", i=RUN, two=2)[:, :, :, :, 1]
+            full = flat.rearrange("p j (c i) -> p c j i", i=RUN)
+            hi = slab["hi"][:, elems].rearrange("p (c i j) -> p c j i", i=RUN, j=PACK)
+            lo = slab["lo"][:, elems].rearrange("p (c i j) -> p c j i", i=RUN, j=PACK)
+            pairs = slab["hi"][:, elems].bitcast(I32)
+            units.append({"upper": upper, "hi": hi, "pairs": pairs, "subs": [(lo, full, hi)], "slab": slab, "cols": cols, "done": cols.stop == slab["cols"]})
 
+        w_slabs = [new_slab("w%d" % g, M) for g in range(PASSES)]
         chunks = []
         c0 = 0
         for c, width in enumerate(CHUNKS):
             groups = [[g] for g in range(PASSES)] if width == SLAB_COLS else [list(range(PASSES))]
             chunk = {"c0": c0, "width": width, "slabs": []}
             for gs in groups:
-                name = "x%d_%d" % (c, gs[0])
-                slab = new_slab(name, width * len(gs))
-                raw = keep.tile([P, PACK, len(gs), width], F32, name=name + "raw", align_bytes=256)
-                for n, g in enumerate(gs):
-                    nc.sync.dma_start(out=raw[:, :, n, :], in_=rows(x, g, c0, width))
-                flat = raw[:].rearrange("p j g c -> p j (g c)")
-                upper = flat.bitcast(BF16).rearrange("p j (c i two) -> p c j i two", i=RUN, two=2)[:, :, :, :, 1]
-                hi = slab["hi"][:].rearrange("p (c i j) -> p c j i", i=RUN, j=PACK)
-                lo = slab["lo"][:].rearrange("p (c i j) -> p c j i", i=RUN, j=PACK)
-                full = flat.rearrange("p j (c i) -> p c j i", i=RUN)
-                slab["parts"].append({"upper": upper, "hi": hi, "pairs": slab["hi"][:].bitcast(I32), "subs": [(lo, full, hi)]})
+                slab = new_slab("x%d_%d" % (c, gs[0]), width * len(gs))
                 slab["passes"] = gs
                 slab["chunk"] = c
-                slabs.append(slab)
                 chunk["slabs"].append(slab)
             chunk["y"] = keep.tile([P, PACK, width], F32, name="y%d" % c, align_bytes=256)
             chunk["y16"] = keep.tile([P, width * PACK], BF16, name="y16_%d" % c, align_bytes=256)
             chunk["codes"] = keep.tile([P, width], U32, name="yc%d" % c, align_bytes=256)
             chunks.append(chunk)
             c0 += width
+
+        units = []
+        first = chunks[0]["slabs"][0]
+        x_load(first, 0, 128)
+        x_load(first, 128, 128)
+        for g in range(PASSES):
+            w_load(g, 0, 256)
+            w_load(g, 256, 256)
+        x_load(first, 256, 256)
+        x_load(chunks[0]["slabs"][1], 0, SLAB_COLS)
+        bias = keep.tile([P, PACK], F32)
+        nc.sync.dma_start(out=bias[:], in_=b.rearrange("(p t) -> p t", t=PACK))
+        for chunk in chunks[1:]:
+            for slab in chunk["slabs"]:
+                x_load(slab, 0, chunk["width"])
         y_scales = keep.tile([P, T], U8, align_bytes=256)
 
         warm_in = keep.tile([P, 1], F32)
@@ -103,9 +118,8 @@ def tile_mix_split3_fm_pl_silu_kernel(tc, w, x, b, out_0, out_1, out_2):
         nc.gpsimd.memset(warm_in[:], 0.0)
         nc.scalar.activation(out=warm_out[:], in_=warm_in[:], func=SILU)
 
-        def take_upper(slab):
-            for part in slab["parts"]:
-                nc.scalar.copy(out=part["hi"], in_=part["upper"])
+        def take_upper(unit, copy):
+            copy(out=unit["hi"], in_=unit["upper"])
 
         def mask(part):
             nc.vector.tensor_scalar(out=part["pairs"], in0=part["pairs"], scalar1=HI_MASK, scalar2=None, op0=ALU.bitwise_and)
@@ -137,15 +151,23 @@ def tile_mix_split3_fm_pl_silu_kernel(tc, w, x, b, out_0, out_1, out_2):
                             stop=(g == PASSES - 1 and half == "lo"),
                         )
 
-        def quantize(slab, half):
-            nc.vector.quantize_mx(out=slab[half + "_codes"][:].bitcast(FP8X4), scales=slab[half + "_scales"][:], in_=slab[half][:])
-            if "chunk" in slab:
+        def quantize(unit, half):
+            slab, cols = unit["slab"], unit["cols"]
+            nc.vector.quantize_mx(
+                out=slab[half + "_codes"][:, cols].bitcast(FP8X4),
+                scales=slab[half + "_scales"][:, cols],
+                in_=slab[half][:, cols.start * PACK : cols.stop * PACK],
+            )
+            if "chunk" in slab and unit["done"]:
                 multiply(slab, half)
 
         def activate(c):
             chunk = chunks[c]
             for t in range(PACK):
                 nc.scalar.activation(out=chunk["y"][:, t, :], in_=chunk["acc"][t][:, : chunk["width"]], func=SILU, bias=bias[:, t : t + 1])
+
+        def store_y(c):
+            chunk = chunks[c]
             nc.sync.dma_start(out=y_rows[:, :, chunk["c0"] : chunk["c0"] + chunk["width"]], in_=chunk["y"][:])
 
         def round_y(c, copy):
@@ -161,44 +183,48 @@ def tile_mix_split3_fm_pl_silu_kernel(tc, w, x, b, out_0, out_1, out_2):
             nc.vector.quantize_mx(out=chunk["codes"][:].bitcast(FP8X4), scales=y_scales[:, cols], in_=chunk["y16"][:])
             nc.sync.dma_start(out=words_out[:, cols], in_=chunk["codes"][:].bitcast(I32))
 
-        late = chunks[3]["slabs"] + chunks[4]["slabs"]
-        for slab in slabs[: len(slabs) - len(late)]:
-            take_upper(slab)
+        late = units[-2:]
+        take_upper(units[0], nc.vector.tensor_copy)
+        for unit in units[1:-2]:
+            take_upper(unit, nc.scalar.copy)
 
-        mask(slabs[0]["parts"][0])
-        for s, slab in enumerate(slabs):
-            parts = slab["parts"]
-            for n, part in enumerate(parts):
-                last = n == len(parts) - 1
-                for sub in part["subs"][:-1]:
-                    subtract(sub)
-                if not last:
-                    mask(parts[n + 1])
-                subtract(part["subs"][-1])
-                if n == len(parts) - 2:
-                    quantize(slab, "hi")
-            following = slabs[s + 1] if s + 1 < len(slabs) else None
+        mask(units[0])
+        for k, unit in enumerate(units):
+            following = units[k + 1] if k + 1 < len(units) else None
+            quantized = unit["cols"] is not None
+            if quantized:
+                quantize(unit, "hi")
+            for sub in unit["subs"][:-1]:
+                subtract(sub)
+            if not quantized:
+                mask(following)
+            subtract(unit["subs"][-1])
+            if not quantized:
+                continue
             if following is not None:
-                mask(following["parts"][0])
-            quantize(slab, "lo")
-            closed = slab["chunk"] if "chunk" in slab and slab["passes"][-1] == PASSES - 1 else None
-            if closed is not None:
-                activate(closed)
+                mask(following)
+            quantize(unit, "lo")
+            slab = unit["slab"]
+            if "chunk" not in slab or not unit["done"] or slab["passes"][-1] != PASSES - 1:
+                continue
+            closed = slab["chunk"]
+            activate(closed)
+            if closed < len(CHUNKS) - 1:
+                store_y(closed)
             if closed == 0:
-                for late_slab in late:
-                    take_upper(late_slab)
+                for late_unit in late:
+                    take_upper(late_unit, nc.scalar.copy)
                 round_y(0, nc.scalar.copy)
             if closed == 1:
                 quantize_y(0)
                 round_y(1, nc.scalar.copy)
             if closed == 3:
                 round_y(2, nc.scalar.copy)
-            if following is not None and len(following["parts"]) == 1:
-                quantize(following, "hi")
 
         quantize_y(1)
         round_y(3, nc.vector.tensor_copy)
         quantize_y(2)
+        store_y(4)
         quantize_y(3)
         round_y(4, nc.vector.tensor_copy)
         quantize_y(4)

@@ -20,8 +20,13 @@ K_PASS = P * PACK
 PASSES = K // K_PASS
 RUN = 4
 HI_MASK = 0xFFF0FFF0 - (1 << 32)
-W_UNIT = [128, 256]
-CHUNKS = [512, 512, 256, 128, 128]
+LOADS = [("x",0,0,0,128),("x",0,0,128,128),("w",0,0,256),("w",0,256,256),("w",1,0,256),("w",1,256,256),("x",0,0,256,256),("x",0,1,0,512),("b",),("x",1,0,0,512),("x",1,1,0,512),("x",2,0,0,256),("x",3,0,0,128),("x",4,0,0,128)]
+W_UNIT=[128,256]
+SPLIT=[]
+CHUNKS=[512,512,256,128,128]
+YSPLIT = [1, 2, 3, 4]
+BEFORE_LAST = [("q", 0), ("w", 0)]
+AFTER = {-1: [("U", 0), ("u", 1), ("u", 2), ("u", 3), ("u", 4), ("u", 5), ("u", 6), ("u", 7), ("u", 8), ("u", 9), ("u", 10), ("u", 11), ("u", 12)], 9: [("a", 0), ("y", 0), ("r", 0), ("u", 13), ("u", 14)], 11: [("a", 1)], 12: [("a", 2), ("r", 2)], 13: [("a", 3), ("r", 3)], 14: [("a", 4), ("r", 4), ("R", 1), ("q", 2), ("w", 2), ("q", 1), ("w", 1), ("q", 3), ("w", 3), ("q", 4), ("w", 4)]}
 SLAB_COLS = 512
 
 
@@ -84,7 +89,7 @@ def tile_mix_split3_fm_pl_silu_kernel(tc, w, x, b, out_0, out_1, out_2):
         chunks = []
         c0 = 0
         for c, width in enumerate(CHUNKS):
-            groups = [[g] for g in range(PASSES)] if width == SLAB_COLS else [list(range(PASSES))]
+            groups = [[g] for g in range(PASSES)] if width == SLAB_COLS or c in SPLIT else [list(range(PASSES))]
             chunk = {"c0": c0, "width": width, "slabs": []}
             for gs in groups:
                 slab = new_slab("x%d_%d" % (c, gs[0]), width * len(gs))
@@ -98,19 +103,14 @@ def tile_mix_split3_fm_pl_silu_kernel(tc, w, x, b, out_0, out_1, out_2):
             c0 += width
 
         units = []
-        first = chunks[0]["slabs"][0]
-        x_load(first, 0, 128)
-        x_load(first, 128, 128)
-        for g in range(PASSES):
-            w_load(g, 0, 256)
-            w_load(g, 256, 256)
-        x_load(first, 256, 256)
-        x_load(chunks[0]["slabs"][1], 0, SLAB_COLS)
         bias = keep.tile([P, PACK], F32)
-        nc.sync.dma_start(out=bias[:], in_=b.rearrange("(p t) -> p t", t=PACK))
-        for chunk in chunks[1:]:
-            for slab in chunk["slabs"]:
-                x_load(slab, 0, chunk["width"])
+        for item in LOADS:
+            if item[0] == "w":
+                w_load(item[1], item[2], item[3])
+            elif item[0] == "x":
+                x_load(chunks[item[1]]["slabs"][item[2]], item[3], item[4])
+            else:
+                nc.sync.dma_start(out=bias[:], in_=b.rearrange("(p t) -> p t", t=PACK))
         y_scales = keep.tile([P, T], U8, align_bytes=256)
 
         warm_in = keep.tile([P, 1], F32)
@@ -165,9 +165,13 @@ def tile_mix_split3_fm_pl_silu_kernel(tc, w, x, b, out_0, out_1, out_2):
             chunk = chunks[c]
             for t in range(PACK):
                 nc.scalar.activation(out=chunk["y"][:, t, :], in_=chunk["acc"][t][:, : chunk["width"]], func=SILU, bias=bias[:, t : t + 1])
+                if c in YSPLIT:
+                    nc.sync.dma_start(out=y_rows[:, t, chunk["c0"] : chunk["c0"] + chunk["width"]], in_=chunk["y"][:, t, :])
 
         def store_y(c):
             chunk = chunks[c]
+            if c in YSPLIT:
+                return
             nc.sync.dma_start(out=y_rows[:, :, chunk["c0"] : chunk["c0"] + chunk["width"]], in_=chunk["y"][:])
 
         def round_y(c, copy):
@@ -181,12 +185,32 @@ def tile_mix_split3_fm_pl_silu_kernel(tc, w, x, b, out_0, out_1, out_2):
             chunk = chunks[c]
             cols = slice(chunk["c0"], chunk["c0"] + chunk["width"])
             nc.vector.quantize_mx(out=chunk["codes"][:].bitcast(FP8X4), scales=y_scales[:, cols], in_=chunk["y16"][:])
+
+        def store_words(c):
+            chunk = chunks[c]
+            cols = slice(chunk["c0"], chunk["c0"] + chunk["width"])
             nc.sync.dma_start(out=words_out[:, cols], in_=chunk["codes"][:].bitcast(I32))
 
-        late = units[-2:]
-        take_upper(units[0], nc.vector.tensor_copy)
-        for unit in units[1:-2]:
-            take_upper(unit, nc.scalar.copy)
+        def run(items):
+            for kind, n in items:
+                if kind == "u":
+                    take_upper(units[n], nc.scalar.copy)
+                elif kind == "a":
+                    activate(n)
+                elif kind == "y":
+                    store_y(n)
+                elif kind == "r":
+                    round_y(n, nc.scalar.copy)
+                elif kind == "R":
+                    round_y(n, nc.vector.tensor_copy)
+                elif kind == "U":
+                    take_upper(units[n], nc.vector.tensor_copy)
+                elif kind == "w":
+                    store_words(n)
+                else:
+                    quantize_y(n)
+
+        run(AFTER.get(-1, []))
 
         mask(units[0])
         for k, unit in enumerate(units):
@@ -200,34 +224,15 @@ def tile_mix_split3_fm_pl_silu_kernel(tc, w, x, b, out_0, out_1, out_2):
                 mask(following)
             subtract(unit["subs"][-1])
             if not quantized:
+                run(AFTER.get(k, []))
                 continue
             if following is not None:
                 mask(following)
+            else:
+                run(BEFORE_LAST)
             quantize(unit, "lo")
-            slab = unit["slab"]
-            if "chunk" not in slab or not unit["done"] or slab["passes"][-1] != PASSES - 1:
-                continue
-            closed = slab["chunk"]
-            activate(closed)
-            if closed < len(CHUNKS) - 1:
-                store_y(closed)
-            if closed == 0:
-                for late_unit in late:
-                    take_upper(late_unit, nc.scalar.copy)
-                round_y(0, nc.scalar.copy)
-            if closed == 1:
-                quantize_y(0)
-                round_y(1, nc.scalar.copy)
-            if closed == 3:
-                round_y(2, nc.scalar.copy)
+            run(AFTER.get(k, []))
 
-        quantize_y(1)
-        round_y(3, nc.vector.tensor_copy)
-        quantize_y(2)
-        store_y(4)
-        quantize_y(3)
-        round_y(4, nc.vector.tensor_copy)
-        quantize_y(4)
         for q in range(4):
             queue = nc.sync if q % 2 == 0 else nc.scalar
             queue.dma_start(out=scales_out[4 * q : 4 * q + 4, :], in_=y_scales[32 * q : 32 * q + 4, :].bitcast(I32))

@@ -18,15 +18,16 @@ P = 128
 PACK = 4
 K_PASS = P * PACK
 PASSES = K // K_PASS
-RUN = 4
+RUN = 2
 HI_MASK = 0xFFF0FFF0 - (1 << 32)
 LOADS = [("x",0,0,0,128),("x",0,0,128,128),("w",0,0,256),("w",0,256,256),("w",1,0,256),("w",1,256,256),("x",0,0,256,256),("x",0,1,0,512),("b",),("x",1,0,0,512),("x",1,1,0,512),("x",2,0,0,256),("x",3,0,0,128),("x",4,0,0,128)]
 W_UNIT=[128,256]
 SPLIT=[]
 CHUNKS=[512,512,256,128,128]
-YSPLIT = [1, 2, 3, 4]
+YSPLIT = []
+WFIRST = {0: 0, 1: 1, 2: 2, 3: 3, 4: 4}
 BEFORE_LAST = [("q", 0), ("w", 0)]
-AFTER = {-1: [("U", 0), ("u", 1), ("u", 2), ("u", 3), ("u", 4), ("u", 5), ("u", 6), ("u", 7), ("u", 8), ("u", 9), ("u", 10), ("u", 11), ("u", 12)], 9: [("a", 0), ("y", 0), ("r", 0), ("u", 13), ("u", 14)], 11: [("a", 1)], 12: [("a", 2), ("r", 2)], 13: [("a", 3), ("r", 3)], 14: [("a", 4), ("r", 4), ("R", 1), ("q", 2), ("w", 2), ("q", 1), ("w", 1), ("q", 3), ("w", 3), ("q", 4), ("w", 4)]}
+AFTER = {-1: [("U", 0), ("u", 1), ("u", 2), ("u", 3), ("u", 4), ("u", 5), ("u", 6), ("u", 7), ("u", 8), ("u", 9), ("u", 10), ("u", 11), ("u", 12)], 9: [("a", 0), ("y", 0), ("r", 0), ("u", 13)], 11: [("a", 1), ("y", 1), ("u", 14)], 12: [("a", 2), ("y", 2), ("r", 2)], 13: [("a", 3), ("y", 3), ("r", 3)], 14: [("a", 4), ("r", 4), ("q", 2), ("w", 2), ("y", 4), ("R", 1), ("q", 3), ("w", 3), ("q", 1), ("w", 1), ("q", 4), ("w", 4)]}
 SLAB_COLS = 512
 
 
@@ -98,7 +99,6 @@ def tile_mix_split3_fm_pl_silu_kernel(tc, w, x, b, out_0, out_1, out_2):
                 chunk["slabs"].append(slab)
             chunk["y"] = keep.tile([P, PACK, width], F32, name="y%d" % c, align_bytes=256)
             chunk["y16"] = keep.tile([P, width * PACK], BF16, name="y16_%d" % c, align_bytes=256)
-            chunk["codes"] = keep.tile([P, width], U32, name="yc%d" % c, align_bytes=256)
             chunks.append(chunk)
             c0 += width
 
@@ -111,6 +111,7 @@ def tile_mix_split3_fm_pl_silu_kernel(tc, w, x, b, out_0, out_1, out_2):
                 x_load(chunks[item[1]]["slabs"][item[2]], item[3], item[4])
             else:
                 nc.sync.dma_start(out=bias[:], in_=b.rearrange("(p t) -> p t", t=PACK))
+        y_codes = keep.tile([P, T], U32, align_bytes=256)
         y_scales = keep.tile([P, T], U8, align_bytes=256)
 
         warm_in = keep.tile([P, 1], F32)
@@ -184,12 +185,13 @@ def tile_mix_split3_fm_pl_silu_kernel(tc, w, x, b, out_0, out_1, out_2):
         def quantize_y(c):
             chunk = chunks[c]
             cols = slice(chunk["c0"], chunk["c0"] + chunk["width"])
-            nc.vector.quantize_mx(out=chunk["codes"][:].bitcast(FP8X4), scales=y_scales[:, cols], in_=chunk["y16"][:])
+            nc.vector.quantize_mx(out=y_codes[:, cols].bitcast(FP8X4), scales=y_scales[:, cols], in_=chunk["y16"][:])
 
         def store_words(c):
-            chunk = chunks[c]
-            cols = slice(chunk["c0"], chunk["c0"] + chunk["width"])
-            nc.sync.dma_start(out=words_out[:, cols], in_=chunk["codes"][:].bitcast(I32))
+            if c not in WFIRST:
+                return
+            cols = slice(chunks[WFIRST[c]]["c0"], chunks[c]["c0"] + chunks[c]["width"])
+            nc.sync.dma_start(out=words_out[:, cols], in_=y_codes[:, cols].bitcast(I32))
 
         def run(items):
             for kind, n in items:

from contextlib import ExitStack

import concourse.mybir as mybir

K, M, T = 1024, 512, 1536
FLOPS = 3 * 2 * K * M * T

F32 = mybir.dt.float32
BF16 = mybir.dt.bfloat16
I32 = mybir.dt.int32
U32 = mybir.dt.uint32
U8 = mybir.dt.uint8
FP8X4 = mybir.dt.float8_e4m3fn_x4
ALU = mybir.AluOpType
SILU = mybir.ActivationFunctionType.Silu

P = 128
PACK = 4
K_PASS = P * PACK
PASSES = K // K_PASS
RUN = 2
HI_MASK = 0xFFF0FFF0 - (1 << 32)
LOADS = [("x",0,0,0,128),("x",0,0,128,128),("w",0,0,256),("w",0,256,256),("w",1,0,256),("w",1,256,256),("x",0,0,256,256),("x",0,1,0,512),("b",),("x",1,0,0,512),("x",1,1,0,512),("x",2,0,0,256),("x",3,0,0,128),("x",4,0,0,128)]
W_UNIT=[128,256]
SPLIT=[]
CHUNKS=[512,512,256,128,128]
YSPLIT = []
WFIRST = {0: 0, 1: 1, 2: 2, 3: 3, 4: 4}
BEFORE_LAST = [("q", 0), ("w", 0)]
AFTER = {-1: [("U", 0), ("u", 1), ("u", 2), ("u", 3), ("u", 4), ("u", 5), ("u", 6), ("u", 7), ("u", 8), ("u", 9), ("u", 10), ("u", 11), ("u", 12)], 9: [("a", 0), ("y", 0), ("r", 0), ("u", 13)], 11: [("a", 1), ("y", 1), ("u", 14)], 12: [("a", 2), ("y", 2), ("r", 2)], 13: [("a", 3), ("y", 3), ("r", 3)], 14: [("a", 4), ("r", 4), ("q", 2), ("w", 2), ("y", 4), ("R", 1), ("q", 3), ("w", 3), ("q", 1), ("w", 1), ("q", 4), ("w", 4)]}
SLAB_COLS = 512


def tile_mix_split3_fm_pl_silu_kernel(tc, w, x, b, out_0, out_1, out_2):
    nc = tc.nc
    y_rows = out_0.rearrange("(p t) c -> p t c", t=PACK)
    words_out = out_1[0].rearrange("p c i -> p (c i)").bitcast(I32)
    scales_out = out_2[0].bitcast(I32)

    with ExitStack() as ctx:
        keep = ctx.enter_context(tc.tile_pool(name="keep", bufs=1))
        psum = ctx.enter_context(tc.psum_pool(name="psum", bufs=2))
        ctx.enter_context(tc.manual_schedule())

        def new_slab(name, cols):
            slab = {"cols": cols}
            for half in ("hi", "lo"):
                slab[half] = keep.tile([P, cols * PACK], BF16, name=name + half, align_bytes=256)
                slab[half + "_codes"] = keep.tile([P, cols], U32, name=name + half + "c", align_bytes=256)
                slab[half + "_scales"] = keep.tile([P, cols], U8, name=name + half + "s", align_bytes=256)
            return slab

        def rows(src, g, c0, width):
            return src[g * K_PASS : (g + 1) * K_PASS, c0 : c0 + width].rearrange("(p j) c -> p j c", j=PACK)

        def w_load(g, c0, width):
            raw = keep.tile([P, PACK, width], F32, name="w%d_%d" % (g, c0), align_bytes=256)
            nc.sync.dma_start(out=raw[:], in_=rows(w, g, c0, width))
            slab = w_slabs[g]
            step = W_UNIT[g]
            for u0 in range(0, width, step):
                m = slice((c0 + u0) // PACK, (c0 + u0 + step) // PACK)
                src = raw[:, :, u0 : u0 + step]
                upper = src.bitcast(BF16).rearrange("p j (m t two) -> p m j t two", t=PACK, two=2)[:, :, :, :, 1]
                full = src.rearrange("p j (m t) -> p m j t", t=PACK)
                hi = slab["hi"][:].rearrange("p (t m j) -> p m j t", t=PACK, j=PACK)[:, m]
                lo = slab["lo"][:].rearrange("p (t m j) -> p m j t", t=PACK, j=PACK)[:, m]
                pairs = slab["hi"][:].bitcast(I32).rearrange("p (t m h) -> p t m h", t=PACK, h=2)[:, :, m, :]
                subs = [(lo[:, :, :, t : t + 2], full[:, :, :, t : t + 2], hi[:, :, :, t : t + 2]) for t in (0, 2)]
                done = c0 + u0 + step == M
                units.append({"upper": upper, "hi": hi, "pairs": pairs, "subs": subs, "slab": slab, "cols": slice(0, M) if done else None, "done": done})

        def x_load(slab, c0, width):
            chunk = chunks[slab["chunk"]]
            gs = slab["passes"]
            raw = keep.tile([P, PACK, len(gs), width], F32, name="x%d_%d" % (gs[0], chunk["c0"] + c0), align_bytes=256)
            for n, g in enumerate(gs):
                nc.sync.dma_start(out=raw[:, :, n, :], in_=rows(x, g, chunk["c0"] + c0, width))
            cols = slice(c0, c0 + width * len(gs))
            elems = slice(cols.start * PACK, cols.stop * PACK)
            flat = raw[:].rearrange("p j g c -> p j (g c)")
            upper = flat.bitcast(BF16).rearrange("p j (c i two) -> p c j i two", i=RUN, two=2)[:, :, :, :, 1]
            full = flat.rearrange("p j (c i) -> p c j i", i=RUN)
            hi = slab["hi"][:, elems].rearrange("p (c i j) -> p c j i", i=RUN, j=PACK)
            lo = slab["lo"][:, elems].rearrange("p (c i j) -> p c j i", i=RUN, j=PACK)
            pairs = slab["hi"][:, elems].bitcast(I32)
            units.append({"upper": upper, "hi": hi, "pairs": pairs, "subs": [(lo, full, hi)], "slab": slab, "cols": cols, "done": cols.stop == slab["cols"]})

        w_slabs = [new_slab("w%d" % g, M) for g in range(PASSES)]
        chunks = []
        c0 = 0
        for c, width in enumerate(CHUNKS):
            groups = [[g] for g in range(PASSES)] if width == SLAB_COLS or c in SPLIT else [list(range(PASSES))]
            chunk = {"c0": c0, "width": width, "slabs": []}
            for gs in groups:
                slab = new_slab("x%d_%d" % (c, gs[0]), width * len(gs))
                slab["passes"] = gs
                slab["chunk"] = c
                chunk["slabs"].append(slab)
            chunk["y"] = keep.tile([P, PACK, width], F32, name="y%d" % c, align_bytes=256)
            chunk["y16"] = keep.tile([P, width * PACK], BF16, name="y16_%d" % c, align_bytes=256)
            chunks.append(chunk)
            c0 += width

        units = []
        bias = keep.tile([P, PACK], F32)
        for item in LOADS:
            if item[0] == "w":
                w_load(item[1], item[2], item[3])
            elif item[0] == "x":
                x_load(chunks[item[1]]["slabs"][item[2]], item[3], item[4])
            else:
                nc.sync.dma_start(out=bias[:], in_=b.rearrange("(p t) -> p t", t=PACK))
        y_codes = keep.tile([P, T], U32, align_bytes=256)
        y_scales = keep.tile([P, T], U8, align_bytes=256)

        warm_in = keep.tile([P, 1], F32)
        warm_out = keep.tile([P, 1], F32)
        nc.gpsimd.memset(warm_in[:], 0.0)
        nc.scalar.activation(out=warm_out[:], in_=warm_in[:], func=SILU)

        def take_upper(unit, copy):
            copy(out=unit["hi"], in_=unit["upper"])

        def mask(part):
            nc.vector.tensor_scalar(out=part["pairs"], in0=part["pairs"], scalar1=HI_MASK, scalar2=None, op0=ALU.bitwise_and)

        def subtract(sub):
            nc.vector.tensor_tensor(out=sub[0], in0=sub[1], in1=sub[2], op=ALU.subtract)

        def multiply(slab, half):
            chunk = chunks[slab["chunk"]]
            width = chunk["width"]
            if half == "hi" and slab["passes"][0] == 0:
                chunk["acc"] = []
                for t in range(PACK):
                    acc = psum.tile([P, SLAB_COLS], F32, name="acc%d" % t)
                    chunk["acc"].append(acc)
            w_halves = ("hi", "lo") if half == "hi" else ("hi",)
            for t in range(PACK):
                n_cols = slice(t * P, (t + 1) * P)
                for n, g in enumerate(slab["passes"]):
                    t_cols = slice(n * width, (n + 1) * width)
                    for w_half in w_halves:
                        nc.tensor.matmul_mx(
                            out=chunk["acc"][t][:, :width],
                            lhsT=w_slabs[g][w_half + "_codes"][:, n_cols].bitcast(FP8X4),
                            lhsT_scale=w_slabs[g][w_half + "_scales"][:, n_cols],
                            rhs=slab[half + "_codes"][:, t_cols].bitcast(FP8X4),
                            rhs_scale=slab[half + "_scales"][:, t_cols],
                            start=(g == 0 and half == "hi" and w_half == "hi"),
                            stop=(g == PASSES - 1 and half == "lo"),
                        )

        def quantize(unit, half):
            slab, cols = unit["slab"], unit["cols"]
            nc.vector.quantize_mx(
                out=slab[half + "_codes"][:, cols].bitcast(FP8X4),
                scales=slab[half + "_scales"][:, cols],
                in_=slab[half][:, cols.start * PACK : cols.stop * PACK],
            )
            if "chunk" in slab and unit["done"]:
                multiply(slab, half)

        def activate(c):
            chunk = chunks[c]
            for t in range(PACK):
                nc.scalar.activation(out=chunk["y"][:, t, :], in_=chunk["acc"][t][:, : chunk["width"]], func=SILU, bias=bias[:, t : t + 1])
                if c in YSPLIT:
                    nc.sync.dma_start(out=y_rows[:, t, chunk["c0"] : chunk["c0"] + chunk["width"]], in_=chunk["y"][:, t, :])

        def store_y(c):
            chunk = chunks[c]
            if c in YSPLIT:
                return
            nc.sync.dma_start(out=y_rows[:, :, chunk["c0"] : chunk["c0"] + chunk["width"]], in_=chunk["y"][:])

        def round_y(c, copy):
            chunk = chunks[c]
            copy(
                out=chunk["y16"][:].rearrange("p (c i t) -> p c t i", i=RUN, t=PACK),
                in_=chunk["y"][:].rearrange("p t (c i) -> p c t i", i=RUN),
            )

        def quantize_y(c):
            chunk = chunks[c]
            cols = slice(chunk["c0"], chunk["c0"] + chunk["width"])
            nc.vector.quantize_mx(out=y_codes[:, cols].bitcast(FP8X4), scales=y_scales[:, cols], in_=chunk["y16"][:])

        def store_words(c):
            if c not in WFIRST:
                return
            cols = slice(chunks[WFIRST[c]]["c0"], chunks[c]["c0"] + chunks[c]["width"])
            nc.sync.dma_start(out=words_out[:, cols], in_=y_codes[:, cols].bitcast(I32))

        def run(items):
            for kind, n in items:
                if kind == "u":
                    take_upper(units[n], nc.scalar.copy)
                elif kind == "a":
                    activate(n)
                elif kind == "y":
                    store_y(n)
                elif kind == "r":
                    round_y(n, nc.scalar.copy)
                elif kind == "R":
                    round_y(n, nc.vector.tensor_copy)
                elif kind == "U":
                    take_upper(units[n], nc.vector.tensor_copy)
                elif kind == "w":
                    store_words(n)
                else:
                    quantize_y(n)

        run(AFTER.get(-1, []))

        mask(units[0])
        for k, unit in enumerate(units):
            following = units[k + 1] if k + 1 < len(units) else None
            quantized = unit["cols"] is not None
            if quantized:
                quantize(unit, "hi")
            for sub in unit["subs"][:-1]:
                subtract(sub)
            if not quantized:
                mask(following)
            subtract(unit["subs"][-1])
            if not quantized:
                run(AFTER.get(k, []))
                continue
            if following is not None:
                mask(following)
            else:
                run(BEFORE_LAST)
            quantize(unit, "lo")
            run(AFTER.get(k, []))

        for q in range(4):
            queue = nc.sync if q % 2 == 0 else nc.scalar
            queue.dma_start(out=scales_out[4 * q : 4 * q + 4, :], in_=y_scales[32 * q : 32 * q + 4, :].bitcast(I32))
